import numpy as np
import ml_dtypes


def mxq(x, axis, fmt="e4m3"):
    dtype, down = {"e4m3": (ml_dtypes.float8_e4m3fn, 7), "e5m2": (ml_dtypes.float8_e5m2, 14)}[fmt]
    v = np.moveaxis(np.asarray(x, np.float32).astype(ml_dtypes.bfloat16).astype(np.float64), axis, -1)
    blocks = v.reshape(v.shape[:-1] + (-1, 32))
    amax = np.abs(blocks).max(-1, keepdims=True)
    byte = np.maximum(np.where(amax > 0, np.frexp(amax)[1] - 1 + 127, 0) - down, 1)
    scale = np.exp2(byte - 127.0)
    codes = (blocks / scale).astype(np.float32).astype(dtype).astype(np.float64)
    return np.moveaxis((codes * scale).reshape(v.shape), -1, axis)


WIDE = False


def mx_kscale(k):
    if not WIDE:
        return np.ones(k)
    levels = np.array([30, -30])
    if k % 512:
        return np.exp2(np.random.permutation(np.resize(levels, k // 32))).repeat(32)
    a = np.empty((k // 512, 16))
    for p in range(k // 512):
        a[p, :8] = np.random.permutation(np.resize(levels, 8))
        for g in range(8):
            far = levels[np.abs(levels - a[p, g]) >= 10]
            a[p, g + 8] = far[np.random.randint(len(far))]
    return np.exp2(a.ravel()).repeat(32)


def f64(x):
    return np.asarray(x).astype(np.float64)


def striped(idx):
    return np.tile(idx.reshape(-1, 16).T, (8, 1)).astype(np.uint16)


def unstriped(offs):
    return offs[:16].T.reshape(-1).astype(np.int64)


def bf(x):
    return np.asarray(x, np.float32).astype(ml_dtypes.bfloat16)


E2M1 = np.array([0.0, 0.5, 1.0, 1.5, 2.0, 3.0, 4.0, 6.0, -0.0, -0.5, -1.0, -1.5, -2.0, -3.0, -4.0, -6.0])


def pack_weight(w, fmt):
    k, n = w.shape
    w = f64(bf(w)).reshape(k // 32, 32, n)
    amax = np.abs(w).max(1)
    if fmt in ("e4m3", "e5m2"):
        byte = np.frexp(amax)[1] - 1 + 127 - (7 if fmt == "e4m3" else 14)
    else:
        mant, ex = np.frexp(amax / 6.0)
        byte = np.where(mant > 0.5, ex, ex - 1) + 127
    byte = np.clip(np.where(amax > 0, byte, 1), 1, 254)
    scaled = (w * np.exp2(127.0 - byte)[:, None, :]).reshape(k, n).astype(np.float32)
    by_word = np.ascontiguousarray(scaled.reshape(k // 512, 128, 4, n).transpose(0, 1, 3, 2))
    if fmt in ("e4m3", "e5m2"):
        words = by_word.astype(ml_dtypes.float8_e4m3fn if fmt == "e4m3" else ml_dtypes.float8_e5m2).view(np.uint8)
    else:
        c = by_word.astype(ml_dtypes.float4_e2m1fn).view(np.uint8) & 0xF
        words = c[..., 0::2] | (c[..., 1::2] << 4)
    return np.ascontiguousarray(words), np.ascontiguousarray(byte.astype(np.uint8).reshape(k // 512, 16, n))


def unpack_weight(words, scales, fmt):
    g, p, n, _ = words.shape
    if fmt in ("e4m3", "e5m2"):
        vals = np.ascontiguousarray(words).view(ml_dtypes.float8_e4m3fn if fmt == "e4m3" else ml_dtypes.float8_e5m2).astype(np.float64)
    else:
        nib = np.empty((g, p, n, 4), np.uint8)
        nib[..., 0::2] = words & 0xF
        nib[..., 1::2] = words >> 4
        vals = E2M1[nib]
    vals = vals * np.repeat(np.exp2(scales.astype(np.float64) - 127.0), 8, axis=1)[..., None]
    return vals.transpose(0, 1, 3, 2).reshape(g * 512, n)


K, H, N, T, S = 1536, 512, 1536, 4096, 1024

def setup_inputs():
    n = np.random.standard_normal
    s = mx_kscale(K)[:, None]
    u = mx_kscale(H)[:, None]
    err = 0.5 * n((K, T)) * np.exp(0.8 * n((1, T)))
    tab_words, tab_scales = pack_weight(err * s, "e5m2")
    w2_words, w2_scales = pack_weight(n((K, H)) / np.sqrt(K) / s, "e4m3")
    return {
        "tab_words": tab_words,
        "tab_scales": tab_scales,
        "offs": striped(np.random.permutation(T)[:S]),
        "w1": (1.5 * n((K, H)) / np.sqrt(K) / s * u.T).astype(np.float32),
        "w2_words": w2_words,
        "w2_scales": w2_scales,
        "bg": (0.7 * n(H)).astype(np.float32),
        "w3": (1.5 * n((H, N)) / np.sqrt(H) / u).astype(np.float32),
        "p": np.random.uniform(0.3, 1.0, S).astype(np.float32),
    }

def reference(tab_words, tab_scales, offs, w1, w2_words, w2_scales, bg, w3, p):
    v = unpack_weight(tab_words, tab_scales, "e5m2")[:, unstriped(offs)]
    w2 = unpack_weight(w2_words, w2_scales, "e4m3")
    a = mxq(f64(w1), 0, "e4m3").T @ v
    b = (w2.T @ v) + f64(bg)[:, None]
    h = a / (1.0 + np.exp(-b))
    g = mxq(f64(w3), 0, "e4m3").T @ mxq(h, 0, "e4m3")
    return g * f64(p)[None, :]

@@ -1,0 +1,282 @@
+from contextlib import ExitStack
+
+import concourse.mybir as mybir
+from concourse.masks import make_identity
+
+K, H, N, T, S = 1536, 512, 1536, 4096, 1024
+FLOPS = 2 * S * (2 * K * H + H * N)
+
+F32 = mybir.dt.float32
+BF16 = mybir.dt.bfloat16
+I32 = mybir.dt.int32
+U32 = mybir.dt.uint32
+U16 = mybir.dt.uint16
+U8 = mybir.dt.uint8
+E4M3 = mybir.dt.float8_e4m3fn_x4
+E5M2 = mybir.dt.float8_e5m2_x4
+MULT = mybir.AluOpType.mult
+SIGMOID = mybir.ActivationFunctionType.Sigmoid
+
+P = 128
+PACK = 4
+PASSES = K // (P * PACK)
+BANK = 512
+HALVES = S // BANK
+CHUNKS = N // BANK
+LIST_COLS = BANK // 16
+
+
+def tile_list_gated_expert_backward_kernel(
+    tc, tab_words, tab_scales, offs, w1, w2_words, w2_scales, bg, w3, p, out
+):
+    nc = tc.nc
+    with ExitStack() as ctx:
+        keep = ctx.enter_context(tc.tile_pool(name="keep", bufs=1))
+        stream = ctx.enter_context(tc.tile_pool(name="stream", bufs=3))
+        work = ctx.enter_context(tc.tile_pool(name="work", bufs=2))
+        stage = ctx.enter_context(tc.tile_pool(name="stage", bufs=4))
+        psum = ctx.enter_context(tc.psum_pool(name="psum", bufs=8))
+
+        def bank():
+            return psum.tile([P, BANK], F32, name="bank")
+
+        offsets = keep.tile([P, S // 16], U16, name="offsets")
+        nc.sync.dma_start(offsets[:], offs)
+
+        scale_rows = tab_scales.rearrange("a q t -> (a q) t").bitcast(I32)
+        scale_win = keep.tile([P, T], U8, name="scale_win", align_bytes=64)
+        scale_win_i = scale_win[:].bitcast(I32)
+        nc.sync.dma_start(scale_win_i[32:64, :], scale_rows[0:32, :])
+        nc.sync.dma_start(scale_win_i[80:96, :], scale_rows[32:48, :])
+        scale_row0 = [32, 48, 80]
+
+        w2_sraw = keep.tile([P, PASSES * H], U8, name="w2_sraw", align_bytes=64)
+        nc.vector.memset(w2_sraw[:].bitcast(I32), 0)
+        for lo, hi in ((0, 32), (64, 80), (96, 128)):
+            nc.vector.memset(scale_win_i[lo:hi, :], 0)
+        v_scales = keep.tile([P, PASSES * S], U8, name="v_scales", align_bytes=64)
+        nc.vector.memset(v_scales[:].bitcast(I32), 0)
+
+        for q in range(4):
+            nc.gpsimd.dma_start(
+                w2_sraw[:].bitcast(I32).rearrange("p (a c) -> p a c", a=PASSES)[32 * q : 32 * q + 4],
+                w2_scales.bitcast(I32)[:, 4 * q : 4 * q + 4, :].rearrange("a r c -> r a c"),
+            )
+
+        bias = keep.tile([P, PACK], F32, name="bias")
+        nc.sync.dma_start(bias[:], bg.rearrange("(p t) -> p t", t=PACK))
+        p_cols = keep.tile([P, HALVES, PACK], F32, name="p_cols")
+        nc.sync.dma_start(p_cols[:], p.rearrange("(h q c) -> q h c", h=HALVES, c=PACK))
+
+        w2_raw = keep.tile([P, PASSES, H], I32, name="w2_raw", align_bytes=64)
+        nc.sync.dma_start(
+            w2_raw[:], w2_words.rearrange("a p c i -> p a (c i)").bitcast(I32)
+        )
+        tabs = []
+        for a in range(PASSES):
+            tab = stream.tile([P, T], U32, name="tab%d" % a, tag="stream", align_bytes=64)
+            nc.sync.dma_start(
+                tab[:].bitcast(I32), tab_words[a].rearrange("p t i -> p (t i)").bitcast(I32)
+            )
+            tabs.append(tab)
+
+        picked = keep.tile([P, S], U8, name="picked", align_bytes=64)
+        nc.vector.tensor_copy(picked[:], scale_win[:].indirect(offsets[:]))
+        for a in range(PASSES):
+            queue = nc.scalar if a == 0 else nc.gpsimd
+            for q in range(4):
+                row = scale_row0[a] + 4 * q
+                queue.dma_start(
+                    v_scales[:].bitcast(I32)[32 * q : 32 * q + 4, a * S // 4 : (a + 1) * S // 4],
+                    picked[:].bitcast(I32)[row : row + 4, :],
+                )
+
+        ident = keep.tile([P, P], F32, name="ident")
+        make_identity(nc, ident[:])
+        p_all = []
+        for h in range(HALVES):
+            acc = bank()
+            for c in range(PACK):
+                nc.tensor.transpose(
+                    acc[:, c * P : (c + 1) * P],
+                    p_cols[:, h, c : c + 1].to_broadcast([P, P]),
+                    ident[:],
+                )
+            ph = keep.tile([P, BANK], F32, name="p_all%d" % h)
+            nc.scalar.copy(
+                ph[:].rearrange("p (q c) -> p q c", c=PACK),
+                acc[:].rearrange("p (c q) -> p q c", c=PACK),
+            )
+            p_all.append(ph)
+        warm = keep.tile([P, 1], F32, name="warm")
+        nc.scalar.activation(warm[:], bias[:, 0:1], SIGMOID)
+
+        w2_codes = keep.tile([P, PASSES * H], I32, name="w2_codes", align_bytes=64)
+        nc.vector.tensor_copy(
+            w2_codes[:].rearrange("p (a t m) -> p a m t", a=PASSES, t=PACK),
+            w2_raw[:].rearrange("p a (m t) -> p a m t", t=PACK),
+        )
+        w2_sc = keep.tile([P, PASSES * H], U8, name="w2_sc", align_bytes=64)
+        nc.vector.tensor_copy(
+            w2_sc[:].rearrange("p (a t m) -> p a m t", a=PASSES, t=PACK),
+            w2_sraw[:].rearrange("p (a m t) -> p a m t", a=PASSES, t=PACK),
+        )
+
+        v_codes = {}
+
+        def gather(a, halves):
+            width = BANK * len(halves)
+            g = keep.tile([P, width], U32, name="v%d_%d" % (a, halves[0]), align_bytes=64)
+            cols = slice(halves[0] * LIST_COLS, (halves[-1] + 1) * LIST_COLS)
+            nc.vector.tensor_copy(g[:], tabs[a][:].indirect(offsets[:, cols]))
+            for i, h in enumerate(halves):
+                v_codes[a, h] = g[:, i * BANK : (i + 1) * BANK]
+
+        def first_pass(acc, codes, scales, a, h):
+            nc.tensor.matmul_mx(
+                out=acc[:],
+                lhsT=codes.bitcast(E4M3),
+                lhsT_scale=scales,
+                rhs=v_codes[a, h].bitcast(E5M2),
+                rhs_scale=v_scales[:, a * S + h * BANK : a * S + (h + 1) * BANK],
+                start=(a == 0),
+                stop=(a == PASSES - 1),
+            )
+
+        b_acc = {}
+        gates = {}
+        for a in range(PASSES):
+            if a < PASSES - 1:
+                gather(a, [0, 1])
+            for h in range(HALVES):
+                if a == PASSES - 1:
+                    gather(a, [h])
+            for h in range(HALVES):
+                for t in range(PACK):
+                    if a == 0:
+                        b_acc[h, t] = bank()
+                    cols = slice(a * H + t * P, a * H + (t + 1) * P)
+                    first_pass(b_acc[h, t], w2_codes[:, cols], w2_sc[:, cols], a, h)
+                    if a == PASSES - 1:
+                        gate = keep.tile([P, BANK], F32, name="gate%d_%d" % (h, t))
+                        nc.scalar.activation(
+                            gate[:], b_acc[h, t][:], SIGMOID, bias=bias[:, t : t + 1]
+                        )
+                        gates[h, t] = gate
+
+        a_acc = {}
+        for a in range(PASSES):
+            raw = stream.tile([P, PACK, H], F32, name="w1_raw%d" % a, tag="stream", align_bytes=64)
+            nc.sync.dma_start(
+                raw[:], w1[a * 512 : (a + 1) * 512, :].rearrange("(p j) c -> p j c", j=PACK)
+            )
+            woven = work.tile([P, PACK * H], BF16, name="w1_woven", align_bytes=64)
+            dst = woven[:].rearrange("p (t m j) -> p m j t", t=PACK, j=PACK)
+            src = raw[:].rearrange("p j (m t) -> p m j t", t=PACK)
+            if a < PASSES - 1:
+                nc.vector.tensor_copy(dst, src)
+            else:
+                nc.vector.tensor_copy(dst[:, 0:80], src[:, 0:80])
+                nc.scalar.copy(dst[:, 80:128], src[:, 80:128])
+            codes = keep.tile([P, H], U32, name="w1_codes%d" % a, align_bytes=64)
+            scales = keep.tile([P, H], U8, name="w1_scales%d" % a, align_bytes=64)
+            nc.vector.quantize_mx(out=codes[:].bitcast(E4M3), scales=scales[:], in_=woven[:])
+            for h in range(HALVES):
+                for t in range(PACK):
+                    if a == 0:
+                        a_acc[h, t] = bank()
+                    cols = slice(t * P, (t + 1) * P)
+                    first_pass(a_acc[h, t], codes[:, cols], scales[:, cols], a, h)
+
+        w3_raw = []
+        for g in range(CHUNKS):
+            raw = stream.tile([P, PACK, BANK], F32, name="w3_raw%d" % g, tag="stream", align_bytes=64)
+            nc.sync.dma_start(
+                raw[:], w3.rearrange("(p j) n -> p j n", j=PACK)[:, :, g * BANK : (g + 1) * BANK]
+            )
+            w3_raw.append(raw)
+
+        w3_woven = {}
+        w3_q = {}
+
+        def weave_w3(g):
+            woven = work.tile([P, PACK * BANK], BF16, name="w3_woven", align_bytes=64)
+            dst = woven[:].rearrange("p (c i j) -> p c j i", i=4, j=PACK)
+            src = w3_raw[g][:].rearrange("p j (c i) -> p c j i", i=4)
+            for lo in (0, 64):
+                nc.scalar.copy(dst[:, lo : lo + 64], src[:, lo : lo + 64])
+            w3_woven[g] = woven
+
+        def quantize(name, woven):
+            codes = keep.tile([P, BANK], U32, name=name + "_codes", align_bytes=64)
+            scales = keep.tile([P, BANK], U8, name=name + "_scales", align_bytes=64)
+            nc.vector.quantize_mx(out=codes[:].bitcast(E4M3), scales=scales[:], in_=woven[:])
+            return codes, scales
+
+        h_woven = {}
+        h_q = {}
+
+        def gate_half(h):
+            hid = work.tile([P, PACK, BANK], BF16, name="hid", align_bytes=64)
+            for t in range(PACK):
+                nc.vector.tensor_tensor(hid[:, t, :], a_acc[h, t][:], gates[h, t][:], MULT)
+            woven = work.tile([P, PACK * BANK], BF16, name="h_woven", align_bytes=64)
+            nc.scalar.copy(
+                woven[:].rearrange("p (c i t) -> p c t i", i=4, t=PACK),
+                hid[:].rearrange("p t (c i) -> p c t i", i=4),
+            )
+            h_woven[h] = woven
+
+        def second(g, nt, h, dst):
+            acc = bank()
+            codes, scales = w3_q[g]
+            cols = slice(nt * P, (nt + 1) * P)
+            nc.tensor.matmul_mx(
+                out=acc[:],
+                lhsT=codes[:, cols].bitcast(E4M3),
+                lhsT_scale=scales[:, cols],
+                rhs=h_q[h][0][:].bitcast(E4M3),
+                rhs_scale=h_q[h][1][:],
+                start=True,
+                stop=True,
+            )
+            nc.vector.tensor_tensor(dst, acc[:], p_all[h][:], MULT)
+
+        def store_half(g, nt, h):
+            res = stage.tile([P, BANK], F32, name="res_half", tag="res")
+            second(g, nt, h, res[:])
+            rows = slice(g * BANK + nt * P, g * BANK + (nt + 1) * P)
+            nc.sync.dma_start(out[rows, h * BANK : (h + 1) * BANK], res[:])
+
+        def store_both(g, nt):
+            res = stage.tile([P, S], F32, name="res_both", tag="res")
+            for h in range(HALVES):
+                second(g, nt, h, res[:, h * BANK : (h + 1) * BANK])
+            rows = slice(g * BANK + nt * P, g * BANK + (nt + 1) * P)
+            nc.sync.dma_start(out[rows, :], res[:])
+
+        weave_w3(0)
+        gate_half(0)
+        gate_half(1)
+        w3_q[0] = quantize("w3_0", w3_woven[0])
+        h_q[0] = quantize("h0", h_woven[0])
+        weave_w3(1)
+        store_half(0, 0, 0)
+        store_half(0, 1, 0)
+        h_q[1] = quantize("h1", h_woven[1])
+        store_half(0, 2, 0)
+        store_half(0, 3, 0)
+        weave_w3(2)
+        store_half(0, 0, 1)
+        store_half(0, 1, 1)
+        w3_q[1] = quantize("w3_1", w3_woven[1])
+        store_half(0, 2, 1)
+        store_half(0, 3, 1)
+        store_both(1, 0)
+        w3_q[2] = quantize("w3_2", w3_woven[2])
+        for nt in range(1, PACK):
+            store_both(1, nt)
+        for nt in range(PACK - 1):
+            store_both(2, nt)
+        for h in range(HALVES):
+            store_half(2, PACK - 1, h)

@@ -15,6 +15,7 @@ U8 = mybir.dt.uint8
 E4M3 = mybir.dt.float8_e4m3fn_x4
 E5M2 = mybir.dt.float8_e5m2_x4
 MULT = mybir.AluOpType.mult
+ADD = mybir.AluOpType.add
 SIGMOID = mybir.ActivationFunctionType.Sigmoid
 
 P = 128
@@ -24,6 +25,14 @@ BANK = 512
 HALVES = S // BANK
 CHUNKS = N // BANK
 LIST_COLS = BANK // 16
+UNIT = 8192
+WIN_AT = 2 * UNIT - T // 2
+TAB_AT = [4 * UNIT, 0, 2 * UNIT]
+W1_AT = [4 * UNIT, 0, UNIT]
+W3_AT = [2 * UNIT, 2 * UNIT + UNIT // 2, 3 * UNIT, 4 * UNIT]
+W3_CHUNKS = [(0, 2), (2, 4), (4, 8), (8, 12)]
+ORDER = [(nt, h) for h in range(2) for nt in range(8)] + [(nt, h) for nt in range(8, 12) for h in range(2)]
+POOL_TILES = ORDER[1:8:2] + ORDER[10:20:3]
 
 
 def tile_list_gated_expert_backward_kernel(
@@ -32,9 +41,9 @@ def tile_list_gated_expert_backward_kernel(
     nc = tc.nc
     with ExitStack() as ctx:
         keep = ctx.enter_context(tc.tile_pool(name="keep", bufs=1))
-        stream = ctx.enter_context(tc.tile_pool(name="stream", bufs=3))
+        stream = ctx.enter_context(tc.tile_pool(name="stream", bufs=1))
         work = ctx.enter_context(tc.tile_pool(name="work", bufs=2))
-        stage = ctx.enter_context(tc.tile_pool(name="stage", bufs=4))
+        stage = ctx.enter_context(tc.tile_pool(name="stage", bufs=8))
         psum = ctx.enter_context(tc.psum_pool(name="psum", bufs=8))
 
         def bank():
@@ -44,55 +53,59 @@ def tile_list_gated_expert_backward_kernel(
         nc.sync.dma_start(offsets[:], offs)
 
         scale_rows = tab_scales.rearrange("a q t -> (a q) t").bitcast(I32)
-        scale_win = keep.tile([P, T], U8, name="scale_win", align_bytes=64)
+        scale_win = stream.tile([P, T], U8, name="scale_win", align_bytes=64, offset=WIN_AT)
         scale_win_i = scale_win[:].bitcast(I32)
         nc.sync.dma_start(scale_win_i[32:64, :], scale_rows[0:32, :])
         nc.sync.dma_start(scale_win_i[80:96, :], scale_rows[32:48, :])
         scale_row0 = [32, 48, 80]
 
         w2_sraw = keep.tile([P, PASSES * H], U8, name="w2_sraw", align_bytes=64)
-        nc.vector.memset(w2_sraw[:].bitcast(I32), 0)
-        for lo, hi in ((0, 32), (64, 80), (96, 128)):
-            nc.vector.memset(scale_win_i[lo:hi, :], 0)
-        v_scales = keep.tile([P, PASSES * S], U8, name="v_scales", align_bytes=64)
-        nc.vector.memset(v_scales[:].bitcast(I32), 0)
-
+        nc.gpsimd.memset(w2_sraw[:].bitcast(I32), 0)
         for q in range(4):
-            nc.gpsimd.dma_start(
+            nc.sync.dma_start(
                 w2_sraw[:].bitcast(I32).rearrange("p (a c) -> p a c", a=PASSES)[32 * q : 32 * q + 4],
                 w2_scales.bitcast(I32)[:, 4 * q : 4 * q + 4, :].rearrange("a r c -> r a c"),
             )
+        nc.vector.memset(scale_win_i[0:32, :], 0)
+        nc.vector.memset(scale_win_i[64:80, :], 0)
+        nc.gpsimd.memset(scale_win_i[96:128, :], 0)
+        v_scales = keep.tile([P, PASSES * S], U8, name="v_scales", align_bytes=64)
+        nc.gpsimd.memset(v_scales[:].bitcast(I32), 0)
 
-        bias = keep.tile([P, PACK], F32, name="bias")
-        nc.sync.dma_start(bias[:], bg.rearrange("(p t) -> p t", t=PACK))
+        ident = keep.tile([P, P], F32, name="ident")
+        make_identity(nc, ident[:])
         p_cols = keep.tile([P, HALVES, PACK], F32, name="p_cols")
-        nc.sync.dma_start(p_cols[:], p.rearrange("(h q c) -> q h c", h=HALVES, c=PACK))
+        nc.gpsimd.dma_start(p_cols[:], p.rearrange("(h q c) -> q h c", h=HALVES, c=PACK))
+        bias = keep.tile([P, PACK], F32, name="bias")
+        nc.gpsimd.dma_start(bias[:], bg.rearrange("(p t) -> p t", t=PACK))
 
-        w2_raw = keep.tile([P, PASSES, H], I32, name="w2_raw", align_bytes=64)
-        nc.sync.dma_start(
-            w2_raw[:], w2_words.rearrange("a p c i -> p a (c i)").bitcast(I32)
-        )
         tabs = []
-        for a in range(PASSES):
-            tab = stream.tile([P, T], U32, name="tab%d" % a, tag="stream", align_bytes=64)
+
+        def load_table(a):
+            tab = stream.tile([P, T], U32, name="tab%d" % a, align_bytes=64, offset=TAB_AT[a])
             nc.sync.dma_start(
                 tab[:].bitcast(I32), tab_words[a].rearrange("p t i -> p (t i)").bitcast(I32)
             )
             tabs.append(tab)
 
+        load_table(0)
+        w2_raw = keep.tile([P, PASSES, H], I32, name="w2_raw", align_bytes=64)
+        nc.sync.dma_start(
+            w2_raw[:], w2_words.rearrange("a p c i -> p a (c i)").bitcast(I32)
+        )
+
         picked = keep.tile([P, S], U8, name="picked", align_bytes=64)
         nc.vector.tensor_copy(picked[:], scale_win[:].indirect(offsets[:]))
         for a in range(PASSES):
-            queue = nc.scalar if a == 0 else nc.gpsimd
             for q in range(4):
                 row = scale_row0[a] + 4 * q
-                queue.dma_start(
+                nc.sync.dma_start(
                     v_scales[:].bitcast(I32)[32 * q : 32 * q + 4, a * S // 4 : (a + 1) * S // 4],
                     picked[:].bitcast(I32)[row : row + 4, :],
                 )
+            if a + 1 < PASSES:
+                load_table(a + 1)
 
-        ident = keep.tile([P, P], F32, name="ident")
-        make_identity(nc, ident[:])
         p_all = []
         for h in range(HALVES):
             acc = bank()
@@ -109,7 +122,7 @@ def tile_list_gated_expert_backward_kernel(
             )
             p_all.append(ph)
         warm = keep.tile([P, 1], F32, name="warm")
-        nc.scalar.activation(warm[:], bias[:, 0:1], SIGMOID)
+        nc.scalar.activation(warm[:], ident[:, 0:1], SIGMOID)
 
         w2_codes = keep.tile([P, PASSES * H], I32, name="w2_codes", align_bytes=64)
         nc.vector.tensor_copy(
@@ -145,6 +158,18 @@ def tile_list_gated_expert_backward_kernel(
 
         b_acc = {}
         gates = {}
+
+        def sigmoid(h, t):
+            if h == 1 and t >= 2:
+                sig = stream.tile(
+                    [P, BANK], F32, name="gate%d_%d" % (h, t), align_bytes=64,
+                    offset=W1_AT[2] + (t - 2) * 2048,
+                )
+            else:
+                sig = keep.tile([P, BANK], F32, name="gate%d_%d" % (h, t))
+            nc.scalar.activation(sig[:], b_acc[h, t][:], SIGMOID, bias=bias[:, t : t + 1])
+            gates[h, t] = sig
+
         for a in range(PASSES):
             if a < PASSES - 1:
                 gather(a, [0, 1])
@@ -157,42 +182,65 @@ def tile_list_gated_expert_backward_kernel(
                         b_acc[h, t] = bank()
                     cols = slice(a * H + t * P, a * H + (t + 1) * P)
                     first_pass(b_acc[h, t], w2_codes[:, cols], w2_sc[:, cols], a, h)
-                    if a == PASSES - 1:
-                        gate = keep.tile([P, BANK], F32, name="gate%d_%d" % (h, t))
-                        nc.scalar.activation(
-                            gate[:], b_acc[h, t][:], SIGMOID, bias=bias[:, t : t + 1]
-                        )
-                        gates[h, t] = gate
+        for t in range(PACK):
+            sigmoid(0, t)
 
         a_acc = {}
+        w1_q = []
+
+        def hidden_pass(a, h):
+            codes, scales = w1_q[a]
+            for t in range(PACK):
+                if a == 0:
+                    a_acc[h, t] = bank()
+                cols = slice(t * P, (t + 1) * P)
+                first_pass(a_acc[h, t], codes[:, cols], scales[:, cols], a, h)
+
         for a in range(PASSES):
-            raw = stream.tile([P, PACK, H], F32, name="w1_raw%d" % a, tag="stream", align_bytes=64)
-            nc.sync.dma_start(
-                raw[:], w1[a * 512 : (a + 1) * 512, :].rearrange("(p j) c -> p j c", j=PACK)
-            )
+            last = a == PASSES - 1
+            parts = 2 if last else 1
+            width = H // parts
             woven = work.tile([P, PACK * H], BF16, name="w1_woven", align_bytes=64)
             dst = woven[:].rearrange("p (t m j) -> p m j t", t=PACK, j=PACK)
-            src = raw[:].rearrange("p j (m t) -> p m j t", t=PACK)
-            if a < PASSES - 1:
-                nc.vector.tensor_copy(dst, src)
-            else:
-                nc.vector.tensor_copy(dst[:, 0:80], src[:, 0:80])
-                nc.scalar.copy(dst[:, 80:128], src[:, 80:128])
+            rows = w1[a * 512 : (a + 1) * 512, :].rearrange("(p j) c -> p j c", j=PACK)
+            if last:
+                sigmoid(1, 0)
+                sigmoid(1, 1)
+            for i in range(parts):
+                raw = stream.tile(
+                    [P, PACK, width], F32, name="w1_raw%d_%d" % (a, i), align_bytes=64,
+                    offset=W1_AT[a] + i * width * 16,
+                )
+                nc.sync.dma_start(raw[:], rows[:, :, i * width : (i + 1) * width])
+                copy = nc.scalar.copy if last and i == 0 else nc.vector.tensor_copy
+                copy(
+                    dst[:, i * width // PACK : (i + 1) * width // PACK],
+                    raw[:].rearrange("p j (m t) -> p m j t", t=PACK),
+                )
+            if last:
+                sigmoid(1, 2)
+                sigmoid(1, 3)
             codes = keep.tile([P, H], U32, name="w1_codes%d" % a, align_bytes=64)
             scales = keep.tile([P, H], U8, name="w1_scales%d" % a, align_bytes=64)
-            nc.vector.quantize_mx(out=codes[:].bitcast(E4M3), scales=scales[:], in_=woven[:])
-            for h in range(HALVES):
-                for t in range(PACK):
-                    if a == 0:
-                        a_acc[h, t] = bank()
-                    cols = slice(t * P, (t + 1) * P)
-                    first_pass(a_acc[h, t], codes[:, cols], scales[:, cols], a, h)
+            for i in range(parts):
+                cols = slice(i * width, (i + 1) * width)
+                nc.vector.quantize_mx(
+                    out=codes[:, cols].bitcast(E4M3),
+                    scales=scales[:, cols],
+                    in_=woven[:, i * width * PACK : (i + 1) * width * PACK],
+                )
+            w1_q.append((codes, scales))
+            hidden_pass(a, 0)
+        for a in range(PASSES):
+            hidden_pass(a, 1)
 
         w3_raw = []
-        for g in range(CHUNKS):
-            raw = stream.tile([P, PACK, BANK], F32, name="w3_raw%d" % g, tag="stream", align_bytes=64)
+        for g, (lo, hi) in enumerate(W3_CHUNKS):
+            raw = stream.tile(
+                [P, PACK, (hi - lo) * P], F32, name="w3_raw%d" % g, align_bytes=64, offset=W3_AT[g]
+            )
             nc.sync.dma_start(
-                raw[:], w3.rearrange("(p j) n -> p j n", j=PACK)[:, :, g * BANK : (g + 1) * BANK]
+                raw[:], w3.rearrange("(p j) n -> p j n", j=PACK)[:, :, lo * P : hi * P]
             )
             w3_raw.append(raw)
 
@@ -200,83 +248,120 @@ def tile_list_gated_expert_backward_kernel(
         w3_q = {}
 
         def weave_w3(g):
-            woven = work.tile([P, PACK * BANK], BF16, name="w3_woven", align_bytes=64)
+            lo, hi = W3_CHUNKS[g]
+            woven = keep.tile([P, PACK * (hi - lo) * P], BF16, name="w3_woven%d" % g, align_bytes=64)
             dst = woven[:].rearrange("p (c i j) -> p c j i", i=4, j=PACK)
             src = w3_raw[g][:].rearrange("p j (c i) -> p c j i", i=4)
-            for lo in (0, 64):
-                nc.scalar.copy(dst[:, lo : lo + 64], src[:, lo : lo + 64])
+            for c0 in range(0, (hi - lo) * P // 4, 32):
+                if g in (0, 3):
+                    nc.scalar.copy(dst[:, c0 : c0 + 32], src[:, c0 : c0 + 32])
+                else:
+                    nc.gpsimd.tensor_scalar(
+                        woven[:].rearrange("p (n j) -> p n j", j=PACK)[:, 4 * c0 : 4 * c0 + 128],
+                        w3_raw[g][:].rearrange("p j n -> p n j")[:, 4 * c0 : 4 * c0 + 128],
+                        1.0, 0.0, MULT, ADD,
+                    )
             w3_woven[g] = woven
 
-        def quantize(name, woven):
-            codes = keep.tile([P, BANK], U32, name=name + "_codes", align_bytes=64)
-            scales = keep.tile([P, BANK], U8, name=name + "_scales", align_bytes=64)
-            nc.vector.quantize_mx(out=codes[:].bitcast(E4M3), scales=scales[:], in_=woven[:])
-            return codes, scales
+        def quantize_w3(g):
+            lo, hi = W3_CHUNKS[g]
+            codes = keep.tile([P, (hi - lo) * P], U32, name="w3_codes%d" % g, align_bytes=64)
+            scales = keep.tile([P, (hi - lo) * P], U8, name="w3_scales%d" % g, align_bytes=64)
+            nc.vector.quantize_mx(out=codes[:].bitcast(E4M3), scales=scales[:], in_=w3_woven[g][:])
+            for nt in range(lo, hi):
+                cols = slice((nt - lo) * P, (nt - lo + 1) * P)
+                w3_q[nt] = (codes[:, cols], scales[:, cols])
 
+        h_codes = [keep.tile([P, BANK], U32, name="h_codes%d" % h, align_bytes=64) for h in range(HALVES)]
+        h_scales = [keep.tile([P, BANK], U8, name="h_scales%d" % h, align_bytes=64) for h in range(HALVES)]
         h_woven = {}
-        h_q = {}
+        hids = {}
 
-        def gate_half(h):
-            hid = work.tile([P, PACK, BANK], BF16, name="hid", align_bytes=64)
+        def gate(h, lo, hi):
+            hid = keep.tile([P, PACK, hi - lo], BF16, name="hid%d_%d" % (h, lo), align_bytes=64)
             for t in range(PACK):
-                nc.vector.tensor_tensor(hid[:, t, :], a_acc[h, t][:], gates[h, t][:], MULT)
-            woven = work.tile([P, PACK * BANK], BF16, name="h_woven", align_bytes=64)
-            nc.scalar.copy(
-                woven[:].rearrange("p (c i t) -> p c t i", i=4, t=PACK),
-                hid[:].rearrange("p t (c i) -> p c t i", i=4),
-            )
-            h_woven[h] = woven
+                nc.vector.tensor_tensor(
+                    hid[:, t, :], a_acc[h, t][:, lo:hi], gates[h, t][:, lo:hi], MULT
+                )
+            hids[h, lo] = hid
 
-        def second(g, nt, h, dst):
+        def weave_h(h, lo, hi):
+            hid = hids[h, lo]
+            woven = keep.tile([P, PACK * (hi - lo)], BF16, name="h_woven%d_%d" % (h, lo), align_bytes=64)
+            dst = woven[:].rearrange("p (c i t) -> p c t i", i=4, t=PACK)
+            src = hid[:].rearrange("p t (c i) -> p c t i", i=4)
+            step = 64 if h == 0 else 32
+            for c0 in range(0, (hi - lo) // 4, step):
+                nc.scalar.copy(dst[:, c0 : c0 + step], src[:, c0 : c0 + step])
+            h_woven[h, lo] = woven
+
+        def quantize_h(h, lo, hi):
+            nc.vector.quantize_mx(
+                out=h_codes[h][:, lo:hi].bitcast(E4M3),
+                scales=h_scales[h][:, lo:hi],
+                in_=h_woven[h, lo][:],
+            )
+
+        def second(nt, h, dst):
             acc = bank()
-            codes, scales = w3_q[g]
-            cols = slice(nt * P, (nt + 1) * P)
             nc.tensor.matmul_mx(
                 out=acc[:],
-                lhsT=codes[:, cols].bitcast(E4M3),
-                lhsT_scale=scales[:, cols],
-                rhs=h_q[h][0][:].bitcast(E4M3),
-                rhs_scale=h_q[h][1][:],
+                lhsT=w3_q[nt][0].bitcast(E4M3),
+                lhsT_scale=w3_q[nt][1],
+                rhs=h_codes[h][:].bitcast(E4M3),
+                rhs_scale=h_scales[h][:],
                 start=True,
                 stop=True,
             )
-            nc.vector.tensor_tensor(dst, acc[:], p_all[h][:], MULT)
+            if (nt, h) in POOL_TILES:
+                plain = work.tile([P, BANK], F32, name="plain", bufs=3)
+                nc.scalar.copy(plain[:], acc[:])
+                nc.gpsimd.tensor_tensor(dst, plain[:], p_all[h][:], MULT)
+            else:
+                nc.vector.tensor_tensor(dst, acc[:], p_all[h][:], MULT)
 
-        def store_half(g, nt, h):
+        def store_half(nt, h):
             res = stage.tile([P, BANK], F32, name="res_half", tag="res")
-            second(g, nt, h, res[:])
-            rows = slice(g * BANK + nt * P, g * BANK + (nt + 1) * P)
-            nc.sync.dma_start(out[rows, h * BANK : (h + 1) * BANK], res[:])
+            second(nt, h, res[:])
+            nc.sync.dma_start(out[nt * P : (nt + 1) * P, h * BANK : (h + 1) * BANK], res[:])
 
-        def store_both(g, nt):
+        def store_both(nt):
             res = stage.tile([P, S], F32, name="res_both", tag="res")
             for h in range(HALVES):
-                second(g, nt, h, res[:, h * BANK : (h + 1) * BANK])
-            rows = slice(g * BANK + nt * P, g * BANK + (nt + 1) * P)
-            nc.sync.dma_start(out[rows, :], res[:])
+                second(nt, h, res[:, h * BANK : (h + 1) * BANK])
+            nc.sync.dma_start(out[nt * P : (nt + 1) * P, :], res[:])
 
-        weave_w3(0)
-        gate_half(0)
-        gate_half(1)
-        w3_q[0] = quantize("w3_0", w3_woven[0])
-        h_q[0] = quantize("h0", h_woven[0])
-        weave_w3(1)
-        store_half(0, 0, 0)
-        store_half(0, 1, 0)
-        h_q[1] = quantize("h1", h_woven[1])
-        store_half(0, 2, 0)
-        store_half(0, 3, 0)
-        weave_w3(2)
-        store_half(0, 0, 1)
-        store_half(0, 1, 1)
-        w3_q[1] = quantize("w3_1", w3_woven[1])
-        store_half(0, 2, 1)
-        store_half(0, 3, 1)
-        store_both(1, 0)
-        w3_q[2] = quantize("w3_2", w3_woven[2])
-        for nt in range(1, PACK):
-            store_both(1, nt)
-        for nt in range(PACK - 1):
-            store_both(2, nt)
+        for g in range(3):
+            weave_w3(g)
+        for lo in (0, 256):
+            gate(0, lo, lo + 256)
+            weave_h(0, lo, lo + 256)
+        quantize_w3(0)
+        quantize_h(0, 0, 256)
+        quantize_h(0, 256, 512)
+        quantize_w3(1)
+        gate(1, 0, 256)
+        store_half(0, 0)
+        store_half(1, 0)
+        quantize_w3(2)
+        gate(1, 256, 512)
+        store_half(2, 0)
+        store_half(3, 0)
+        weave_h(1, 0, 256)
+        store_half(4, 0)
+        store_half(5, 0)
+        weave_h(1, 256, 512)
+        quantize_h(1, 0, 256)
+        store_half(6, 0)
+        store_half(7, 0)
+        quantize_h(1, 256, 512)
+        for nt in range(6):
+            store_half(nt, 1)
+        weave_w3(3)
+        quantize_w3(3)
+        for nt in range(6, 8):
+            store_half(nt, 1)
+        for nt in range(8, 11):
+            store_both(nt)
         for h in range(HALVES):
-            store_half(2, PACK - 1, h)
+            store_half(11, h)

@@ -29,10 +29,7 @@ UNIT = 8192
 WIN_AT = 2 * UNIT - T // 2
 TAB_AT = [4 * UNIT, 0, 2 * UNIT]
 W1_AT = [4 * UNIT, 0, UNIT]
-W3_AT = [2 * UNIT, 2 * UNIT + UNIT // 2, 3 * UNIT, 4 * UNIT]
-W3_CHUNKS = [(0, 2), (2, 4), (4, 8), (8, 12)]
-ORDER = [(nt, h) for h in range(2) for nt in range(8)] + [(nt, h) for nt in range(8, 12) for h in range(2)]
-POOL_TILES = ORDER[1:8:2] + ORDER[10:20:3]
+W3_AT = [2 * UNIT, 3 * UNIT, 4 * UNIT]
 
 
 def tile_list_gated_expert_backward_kernel(
@@ -202,24 +199,22 @@ def tile_list_gated_expert_backward_kernel(
             width = H // parts
             woven = work.tile([P, PACK * H], BF16, name="w1_woven", align_bytes=64)
             dst = woven[:].rearrange("p (t m j) -> p m j t", t=PACK, j=PACK)
-            rows = w1[a * 512 : (a + 1) * 512, :].rearrange("(p j) c -> p j c", j=PACK)
+            raw = stream.tile(
+                [P, PACK, H], F32, name="w1_raw%d" % a, align_bytes=64, offset=W1_AT[a]
+            )
+            nc.sync.dma_start(
+                raw[:], w1[a * 512 : (a + 1) * 512, :].rearrange("(p j) c -> p j c", j=PACK)
+            )
+            src = raw[:].rearrange("p j (m t) -> p m j t", t=PACK)
             if last:
                 sigmoid(1, 0)
                 sigmoid(1, 1)
-            for i in range(parts):
-                raw = stream.tile(
-                    [P, PACK, width], F32, name="w1_raw%d_%d" % (a, i), align_bytes=64,
-                    offset=W1_AT[a] + i * width * 16,
-                )
-                nc.sync.dma_start(raw[:], rows[:, :, i * width : (i + 1) * width])
-                copy = nc.scalar.copy if last and i == 0 else nc.vector.tensor_copy
-                copy(
-                    dst[:, i * width // PACK : (i + 1) * width // PACK],
-                    raw[:].rearrange("p j (m t) -> p m j t", t=PACK),
-                )
-            if last:
+                nc.vector.tensor_copy(dst[:, :88], src[:, :88])
+                nc.scalar.copy(dst[:, 88:], src[:, 88:])
                 sigmoid(1, 2)
                 sigmoid(1, 3)
+            else:
+                nc.vector.tensor_copy(dst, src)
             codes = keep.tile([P, H], U32, name="w1_codes%d" % a, align_bytes=64)
             scales = keep.tile([P, H], U8, name="w1_scales%d" % a, align_bytes=64)
             for i in range(parts):
@@ -235,39 +230,29 @@ def tile_list_gated_expert_backward_kernel(
             hidden_pass(a, 1)
 
         w3_raw = []
-        for g, (lo, hi) in enumerate(W3_CHUNKS):
+        for g in range(CHUNKS):
             raw = stream.tile(
-                [P, PACK, (hi - lo) * P], F32, name="w3_raw%d" % g, align_bytes=64, offset=W3_AT[g]
+                [P, PACK, BANK], F32, name="w3_raw%d" % g, align_bytes=64, offset=W3_AT[g]
             )
             nc.sync.dma_start(
-                raw[:], w3.rearrange("(p j) n -> p j n", j=PACK)[:, :, lo * P : hi * P]
+                raw[:], w3.rearrange("(p j) n -> p j n", j=PACK)[:, :, g * BANK : (g + 1) * BANK]
             )
             w3_raw.append(raw)
 
         w3_woven = {}
         w3_q = {}
 
-        def weave_w3(g):
-            lo, hi = W3_CHUNKS[g]
-            woven = keep.tile([P, PACK * (hi - lo) * P], BF16, name="w3_woven%d" % g, align_bytes=64)
+        def weave_w3(lo, hi):
+            woven = keep.tile([P, PACK * (hi - lo) * P], BF16, name="w3_woven%d" % lo, align_bytes=64)
             dst = woven[:].rearrange("p (c i j) -> p c j i", i=4, j=PACK)
-            src = w3_raw[g][:].rearrange("p j (c i) -> p c j i", i=4)
-            for c0 in range(0, (hi - lo) * P // 4, 32):
-                if g in (0, 3):
-                    nc.scalar.copy(dst[:, c0 : c0 + 32], src[:, c0 : c0 + 32])
-                else:
-                    nc.gpsimd.tensor_scalar(
-                        woven[:].rearrange("p (n j) -> p n j", j=PACK)[:, 4 * c0 : 4 * c0 + 128],
-                        w3_raw[g][:].rearrange("p j n -> p n j")[:, 4 * c0 : 4 * c0 + 128],
-                        1.0, 0.0, MULT, ADD,
-                    )
-            w3_woven[g] = woven
+            src = w3_raw[lo // 4][:, :, (lo % 4) * P : (lo % 4 + hi - lo) * P]
+            nc.scalar.copy(dst, src.rearrange("p j (c i) -> p c j i", i=4))
+            w3_woven[lo] = woven
 
-        def quantize_w3(g):
-            lo, hi = W3_CHUNKS[g]
-            codes = keep.tile([P, (hi - lo) * P], U32, name="w3_codes%d" % g, align_bytes=64)
-            scales = keep.tile([P, (hi - lo) * P], U8, name="w3_scales%d" % g, align_bytes=64)
-            nc.vector.quantize_mx(out=codes[:].bitcast(E4M3), scales=scales[:], in_=w3_woven[g][:])
+        def quantize_w3(lo, hi):
+            codes = keep.tile([P, (hi - lo) * P], U32, name="w3_codes%d" % lo, align_bytes=64)
+            scales = keep.tile([P, (hi - lo) * P], U8, name="w3_scales%d" % lo, align_bytes=64)
+            nc.vector.quantize_mx(out=codes[:].bitcast(E4M3), scales=scales[:], in_=w3_woven[lo][:])
             for nt in range(lo, hi):
                 cols = slice((nt - lo) * P, (nt - lo + 1) * P)
                 w3_q[nt] = (codes[:, cols], scales[:, cols])
@@ -290,9 +275,7 @@ def tile_list_gated_expert_backward_kernel(
             woven = keep.tile([P, PACK * (hi - lo)], BF16, name="h_woven%d_%d" % (h, lo), align_bytes=64)
             dst = woven[:].rearrange("p (c i t) -> p c t i", i=4, t=PACK)
             src = hid[:].rearrange("p t (c i) -> p c t i", i=4)
-            step = 64 if h == 0 else 32
-            for c0 in range(0, (hi - lo) // 4, step):
-                nc.scalar.copy(dst[:, c0 : c0 + step], src[:, c0 : c0 + step])
+            nc.scalar.copy(dst, src)
             h_woven[h, lo] = woven
 
         def quantize_h(h, lo, hi):
@@ -313,12 +296,7 @@ def tile_list_gated_expert_backward_kernel(
                 start=True,
                 stop=True,
             )
-            if (nt, h) in POOL_TILES:
-                plain = work.tile([P, BANK], F32, name="plain", bufs=3)
-                nc.scalar.copy(plain[:], acc[:])
-                nc.gpsimd.tensor_tensor(dst, plain[:], p_all[h][:], MULT)
-            else:
-                nc.vector.tensor_tensor(dst, acc[:], p_all[h][:], MULT)
+            nc.vector.tensor_tensor(dst, acc[:], p_all[h][:], MULT)
 
         def store_half(nt, h):
             res = stage.tile([P, BANK], F32, name="res_half", tag="res")
@@ -331,37 +309,30 @@ def tile_list_gated_expert_backward_kernel(
                 second(nt, h, res[:, h * BANK : (h + 1) * BANK])
             nc.sync.dma_start(out[nt * P : (nt + 1) * P, :], res[:])
 
-        for g in range(3):
-            weave_w3(g)
+        weave_w3(0, 2)
         for lo in (0, 256):
             gate(0, lo, lo + 256)
             weave_h(0, lo, lo + 256)
-        quantize_w3(0)
+        quantize_w3(0, 2)
         quantize_h(0, 0, 256)
         quantize_h(0, 256, 512)
-        quantize_w3(1)
-        gate(1, 0, 256)
+        weave_w3(2, 4)
+        gate(1, 0, 512)
+        weave_h(1, 0, 512)
+        weave_w3(4, 8)
+        weave_w3(8, 12)
         store_half(0, 0)
-        store_half(1, 0)
-        quantize_w3(2)
-        gate(1, 256, 512)
-        store_half(2, 0)
-        store_half(3, 0)
-        weave_h(1, 0, 256)
-        store_half(4, 0)
-        store_half(5, 0)
-        weave_h(1, 256, 512)
-        quantize_h(1, 0, 256)
-        store_half(6, 0)
-        store_half(7, 0)
-        quantize_h(1, 256, 512)
-        for nt in range(6):
+        quantize_w3(2, 4)
+        for nt in range(1, 4):
+            store_half(nt, 0)
+        quantize_h(1, 0, 512)
+        for nt in range(4):
             store_half(nt, 1)
-        weave_w3(3)
-        quantize_w3(3)
-        for nt in range(6, 8):
-            store_half(nt, 1)
-        for nt in range(8, 11):
+        quantize_w3(4, 8)
+        store_both(4)
+        store_both(5)
+        quantize_w3(8, 12)
+        for nt in range(6, 11):
             store_both(nt)
         for h in range(HALVES):
             store_half(11, h)

@@ -15,21 +15,33 @@ U8 = mybir.dt.uint8
 E4M3 = mybir.dt.float8_e4m3fn_x4
 E5M2 = mybir.dt.float8_e5m2_x4
 MULT = mybir.AluOpType.mult
-ADD = mybir.AluOpType.add
 SIGMOID = mybir.ActivationFunctionType.Sigmoid
 
 P = 128
 PACK = 4
-PASSES = K // (P * PACK)
+K_PASS = P * PACK
+PASSES = K // K_PASS
 BANK = 512
 HALVES = S // BANK
-CHUNKS = N // BANK
+QUADRANTS = 4
+SCALE_ROWS = 4
+LINE = 4
 LIST_COLS = BANK // 16
+ROW_TILES = N // P
+TILES_PER_LOAD = BANK // P
+W3_LOADS = N // BANK
+
+SCALE_ROW0 = [32, 48, 80]
+
 UNIT = 8192
 WIN_AT = 2 * UNIT - T // 2
 TAB_AT = [4 * UNIT, 0, 2 * UNIT]
 W1_AT = [4 * UNIT, 0, UNIT]
 W3_AT = [2 * UNIT, 3 * UNIT, 4 * UNIT]
+
+W1_VECTOR_SHARE = 88
+PIECE = BANK // 2
+LATE_GATES = 2
 
 
 def tile_list_gated_expert_backward_kernel(
@@ -49,19 +61,22 @@ def tile_list_gated_expert_backward_kernel(
         offsets = keep.tile([P, S // 16], U16, name="offsets")
         nc.sync.dma_start(offsets[:], offs)
 
-        scale_rows = tab_scales.rearrange("a q t -> (a q) t").bitcast(I32)
+        scale_rows = tab_scales.rearrange("a q tok -> (a q) tok").bitcast(I32)
         scale_win = stream.tile([P, T], U8, name="scale_win", align_bytes=64, offset=WIN_AT)
         scale_win_i = scale_win[:].bitcast(I32)
         nc.sync.dma_start(scale_win_i[32:64, :], scale_rows[0:32, :])
         nc.sync.dma_start(scale_win_i[80:96, :], scale_rows[32:48, :])
-        scale_row0 = [32, 48, 80]
 
         w2_sraw = keep.tile([P, PASSES * H], U8, name="w2_sraw", align_bytes=64)
         nc.gpsimd.memset(w2_sraw[:].bitcast(I32), 0)
-        for q in range(4):
+        for quad in range(QUADRANTS):
             nc.sync.dma_start(
-                w2_sraw[:].bitcast(I32).rearrange("p (a c) -> p a c", a=PASSES)[32 * q : 32 * q + 4],
-                w2_scales.bitcast(I32)[:, 4 * q : 4 * q + 4, :].rearrange("a r c -> r a c"),
+                w2_sraw[:].bitcast(I32).rearrange("part (a c) -> part a c", a=PASSES)[
+                    32 * quad : 32 * quad + SCALE_ROWS
+                ],
+                w2_scales.bitcast(I32)[:, SCALE_ROWS * quad : SCALE_ROWS * (quad + 1), :].rearrange(
+                    "a row c -> row a c"
+                ),
             )
         nc.vector.memset(scale_win_i[0:32, :], 0)
         nc.vector.memset(scale_win_i[64:80, :], 0)
@@ -72,83 +87,82 @@ def tile_list_gated_expert_backward_kernel(
         ident = keep.tile([P, P], F32, name="ident")
         make_identity(nc, ident[:])
         p_cols = keep.tile([P, HALVES, PACK], F32, name="p_cols")
-        nc.gpsimd.dma_start(p_cols[:], p.rearrange("(h q c) -> q h c", h=HALVES, c=PACK))
+        nc.gpsimd.dma_start(p_cols[:], p.rearrange("(half part c) -> part half c", half=HALVES, c=PACK))
         bias = keep.tile([P, PACK], F32, name="bias")
-        nc.gpsimd.dma_start(bias[:], bg.rearrange("(p t) -> p t", t=PACK))
+        nc.gpsimd.dma_start(bias[:], bg.rearrange("(m t) -> m t", t=PACK))
 
         tabs = []
 
         def load_table(a):
             tab = stream.tile([P, T], U32, name="tab%d" % a, align_bytes=64, offset=TAB_AT[a])
             nc.sync.dma_start(
-                tab[:].bitcast(I32), tab_words[a].rearrange("p t i -> p (t i)").bitcast(I32)
+                tab[:].bitcast(I32), tab_words[a].rearrange("part tok i -> part (tok i)").bitcast(I32)
             )
             tabs.append(tab)
 
         load_table(0)
         w2_raw = keep.tile([P, PASSES, H], I32, name="w2_raw", align_bytes=64)
-        nc.sync.dma_start(
-            w2_raw[:], w2_words.rearrange("a p c i -> p a (c i)").bitcast(I32)
-        )
+        nc.sync.dma_start(w2_raw[:], w2_words.rearrange("a part c i -> part a (c i)").bitcast(I32))
 
         picked = keep.tile([P, S], U8, name="picked", align_bytes=64)
         nc.vector.tensor_copy(picked[:], scale_win[:].indirect(offsets[:]))
         for a in range(PASSES):
-            for q in range(4):
-                row = scale_row0[a] + 4 * q
+            for quad in range(QUADRANTS):
+                row = SCALE_ROW0[a] + SCALE_ROWS * quad
                 nc.sync.dma_start(
-                    v_scales[:].bitcast(I32)[32 * q : 32 * q + 4, a * S // 4 : (a + 1) * S // 4],
-                    picked[:].bitcast(I32)[row : row + 4, :],
+                    v_scales[:].bitcast(I32)[
+                        32 * quad : 32 * quad + SCALE_ROWS, a * S // 4 : (a + 1) * S // 4
+                    ],
+                    picked[:].bitcast(I32)[row : row + SCALE_ROWS, :],
                 )
             if a + 1 < PASSES:
                 load_table(a + 1)
 
         p_all = []
-        for h in range(HALVES):
-            acc = bank()
+        for half in range(HALVES):
+            spread = bank()
             for c in range(PACK):
                 nc.tensor.transpose(
-                    acc[:, c * P : (c + 1) * P],
-                    p_cols[:, h, c : c + 1].to_broadcast([P, P]),
+                    spread[:, c * P : (c + 1) * P],
+                    p_cols[:, half, c : c + 1].to_broadcast([P, P]),
                     ident[:],
                 )
-            ph = keep.tile([P, BANK], F32, name="p_all%d" % h)
+            p_half = keep.tile([P, BANK], F32, name="p_all%d" % half)
             nc.scalar.copy(
-                ph[:].rearrange("p (q c) -> p q c", c=PACK),
-                acc[:].rearrange("p (c q) -> p q c", c=PACK),
+                p_half[:].rearrange("part (n c) -> part n c", c=PACK),
+                spread[:].rearrange("part (c n) -> part n c", c=PACK),
             )
-            p_all.append(ph)
-        warm = keep.tile([P, 1], F32, name="warm")
-        nc.scalar.activation(warm[:], ident[:, 0:1], SIGMOID)
+            p_all.append(p_half)
 
         w2_codes = keep.tile([P, PASSES * H], I32, name="w2_codes", align_bytes=64)
         nc.vector.tensor_copy(
-            w2_codes[:].rearrange("p (a t m) -> p a m t", a=PASSES, t=PACK),
-            w2_raw[:].rearrange("p a (m t) -> p a m t", t=PACK),
+            w2_codes[:].rearrange("part (a t m) -> part a m t", a=PASSES, t=PACK),
+            w2_raw[:].rearrange("part a (m t) -> part a m t", t=PACK),
         )
         w2_sc = keep.tile([P, PASSES * H], U8, name="w2_sc", align_bytes=64)
         nc.vector.tensor_copy(
-            w2_sc[:].rearrange("p (a t m) -> p a m t", a=PASSES, t=PACK),
-            w2_sraw[:].rearrange("p (a m t) -> p a m t", a=PASSES, t=PACK),
+            w2_sc[:].rearrange("part (a t m) -> part a m t", a=PASSES, t=PACK),
+            w2_sraw[:].rearrange("part (a m t) -> part a m t", a=PASSES, t=PACK),
         )
 
         v_codes = {}
 
         def gather(a, halves):
-            width = BANK * len(halves)
-            g = keep.tile([P, width], U32, name="v%d_%d" % (a, halves[0]), align_bytes=64)
-            cols = slice(halves[0] * LIST_COLS, (halves[-1] + 1) * LIST_COLS)
-            nc.vector.tensor_copy(g[:], tabs[a][:].indirect(offsets[:, cols]))
-            for i, h in enumerate(halves):
-                v_codes[a, h] = g[:, i * BANK : (i + 1) * BANK]
+            words = keep.tile(
+                [P, BANK * len(halves)], U32, name="v%d_%d" % (a, halves[0]), align_bytes=64
+            )
+            entries = slice(halves[0] * LIST_COLS, (halves[-1] + 1) * LIST_COLS)
+            nc.vector.tensor_copy(words[:], tabs[a][:].indirect(offsets[:, entries]))
+            for place, half in enumerate(halves):
+                v_codes[a, half] = words[:, place * BANK : (place + 1) * BANK]
 
-        def first_pass(acc, codes, scales, a, h):
+        def table_pass(acc, codes, scales, a, half):
             nc.tensor.matmul_mx(
                 out=acc[:],
                 lhsT=codes.bitcast(E4M3),
                 lhsT_scale=scales,
-                rhs=v_codes[a, h].bitcast(E5M2),
-                rhs_scale=v_scales[:, a * S + h * BANK : a * S + (h + 1) * BANK],
+                rhs=v_codes[a, half].bitcast(E5M2),
+                rhs_scale=v_scales[:, a * S + half * BANK : a * S + (half + 1) * BANK],
                 start=(a == 0),
                 stop=(a == PASSES - 1),
             )
@@ -156,73 +170,68 @@ def tile_list_gated_expert_backward_kernel(
         b_acc = {}
         gates = {}
 
-        def sigmoid(h, t):
-            if h == 1 and t >= 2:
-                sig = stream.tile(
-                    [P, BANK], F32, name="gate%d_%d" % (h, t), align_bytes=64,
-                    offset=W1_AT[2] + (t - 2) * 2048,
-                )
+        def sigmoid(half, t):
+            name = "gate%d_%d" % (half, t)
+            if half == HALVES - 1 and t >= LATE_GATES:
+                at = W1_AT[PASSES - 1] + (t - LATE_GATES) * BANK * 4
+                gate = stream.tile([P, BANK], F32, name=name, align_bytes=64, offset=at)
             else:
-                sig = keep.tile([P, BANK], F32, name="gate%d_%d" % (h, t))
-            nc.scalar.activation(sig[:], b_acc[h, t][:], SIGMOID, bias=bias[:, t : t + 1])
-            gates[h, t] = sig
+                gate = keep.tile([P, BANK], F32, name=name)
+            nc.scalar.activation(gate[:], b_acc[half, t][:], SIGMOID, bias=bias[:, t : t + 1])
+            gates[half, t] = gate
 
         for a in range(PASSES):
             if a < PASSES - 1:
-                gather(a, [0, 1])
-            for h in range(HALVES):
-                if a == PASSES - 1:
-                    gather(a, [h])
-            for h in range(HALVES):
+                gather(a, list(range(HALVES)))
+            else:
+                for half in range(HALVES):
+                    gather(a, [half])
+            for half in range(HALVES):
                 for t in range(PACK):
                     if a == 0:
-                        b_acc[h, t] = bank()
+                        b_acc[half, t] = bank()
                     cols = slice(a * H + t * P, a * H + (t + 1) * P)
-                    first_pass(b_acc[h, t], w2_codes[:, cols], w2_sc[:, cols], a, h)
+                    table_pass(b_acc[half, t], w2_codes[:, cols], w2_sc[:, cols], a, half)
         for t in range(PACK):
             sigmoid(0, t)
 
         a_acc = {}
         w1_q = []
 
-        def hidden_pass(a, h):
+        def hidden_pass(a, half):
             codes, scales = w1_q[a]
             for t in range(PACK):
                 if a == 0:
-                    a_acc[h, t] = bank()
+                    a_acc[half, t] = bank()
                 cols = slice(t * P, (t + 1) * P)
-                first_pass(a_acc[h, t], codes[:, cols], scales[:, cols], a, h)
+                table_pass(a_acc[half, t], codes[:, cols], scales[:, cols], a, half)
 
         for a in range(PASSES):
             last = a == PASSES - 1
-            parts = 2 if last else 1
-            width = H // parts
             woven = work.tile([P, PACK * H], BF16, name="w1_woven", align_bytes=64)
-            dst = woven[:].rearrange("p (t m j) -> p m j t", t=PACK, j=PACK)
-            raw = stream.tile(
-                [P, PACK, H], F32, name="w1_raw%d" % a, align_bytes=64, offset=W1_AT[a]
-            )
+            dst = woven[:].rearrange("part (t m j) -> part m j t", t=PACK, j=PACK)
+            raw = stream.tile([P, PACK, H], F32, name="w1_raw%d" % a, align_bytes=64, offset=W1_AT[a])
             nc.sync.dma_start(
-                raw[:], w1[a * 512 : (a + 1) * 512, :].rearrange("(p j) c -> p j c", j=PACK)
+                raw[:], w1[a * K_PASS : (a + 1) * K_PASS, :].rearrange("(part j) c -> part j c", j=PACK)
             )
-            src = raw[:].rearrange("p j (m t) -> p m j t", t=PACK)
+            src = raw[:].rearrange("part j (m t) -> part m j t", t=PACK)
             if last:
-                sigmoid(1, 0)
-                sigmoid(1, 1)
-                nc.vector.tensor_copy(dst[:, :88], src[:, :88])
-                nc.scalar.copy(dst[:, 88:], src[:, 88:])
-                sigmoid(1, 2)
-                sigmoid(1, 3)
+                for t in range(LATE_GATES):
+                    sigmoid(1, t)
+                nc.vector.tensor_copy(dst[:, :W1_VECTOR_SHARE], src[:, :W1_VECTOR_SHARE])
+                nc.scalar.copy(dst[:, W1_VECTOR_SHARE:], src[:, W1_VECTOR_SHARE:])
+                for t in range(LATE_GATES, PACK):
+                    sigmoid(1, t)
             else:
                 nc.vector.tensor_copy(dst, src)
             codes = keep.tile([P, H], U32, name="w1_codes%d" % a, align_bytes=64)
             scales = keep.tile([P, H], U8, name="w1_scales%d" % a, align_bytes=64)
-            for i in range(parts):
-                cols = slice(i * width, (i + 1) * width)
+            width = H // 2 if last else H
+            for c0 in range(0, H, width):
                 nc.vector.quantize_mx(
-                    out=codes[:, cols].bitcast(E4M3),
-                    scales=scales[:, cols],
-                    in_=woven[:, i * width * PACK : (i + 1) * width * PACK],
+                    out=codes[:, c0 : c0 + width].bitcast(E4M3),
+                    scales=scales[:, c0 : c0 + width],
+                    in_=woven[:, c0 * PACK : (c0 + width) * PACK],
                 )
             w1_q.append((codes, scales))
             hidden_pass(a, 0)
@@ -230,12 +239,10 @@ def tile_list_gated_expert_backward_kernel(
             hidden_pass(a, 1)
 
         w3_raw = []
-        for g in range(CHUNKS):
-            raw = stream.tile(
-                [P, PACK, BANK], F32, name="w3_raw%d" % g, align_bytes=64, offset=W3_AT[g]
-            )
+        for g in range(W3_LOADS):
+            raw = stream.tile([P, PACK, BANK], F32, name="w3_raw%d" % g, align_bytes=64, offset=W3_AT[g])
             nc.sync.dma_start(
-                raw[:], w3.rearrange("(p j) n -> p j n", j=PACK)[:, :, g * BANK : (g + 1) * BANK]
+                raw[:], w3.rearrange("(part j) n -> part j n", j=PACK)[:, :, g * BANK : (g + 1) * BANK]
             )
             w3_raw.append(raw)
 
@@ -244,9 +251,12 @@ def tile_list_gated_expert_backward_kernel(
 
         def weave_w3(lo, hi):
             woven = keep.tile([P, PACK * (hi - lo) * P], BF16, name="w3_woven%d" % lo, align_bytes=64)
-            dst = woven[:].rearrange("p (c i j) -> p c j i", i=4, j=PACK)
-            src = w3_raw[lo // 4][:, :, (lo % 4) * P : (lo % 4 + hi - lo) * P]
-            nc.scalar.copy(dst, src.rearrange("p j (c i) -> p c j i", i=4))
+            first = (lo % TILES_PER_LOAD) * P
+            src = w3_raw[lo // TILES_PER_LOAD][:, :, first : first + (hi - lo) * P]
+            nc.scalar.copy(
+                woven[:].rearrange("part (c i j) -> part c j i", i=LINE, j=PACK),
+                src.rearrange("part j (c i) -> part c j i", i=LINE),
+            )
             w3_woven[lo] = woven
 
         def quantize_w3(lo, hi):
@@ -257,82 +267,96 @@ def tile_list_gated_expert_backward_kernel(
                 cols = slice((nt - lo) * P, (nt - lo + 1) * P)
                 w3_q[nt] = (codes[:, cols], scales[:, cols])
 
-        h_codes = [keep.tile([P, BANK], U32, name="h_codes%d" % h, align_bytes=64) for h in range(HALVES)]
-        h_scales = [keep.tile([P, BANK], U8, name="h_scales%d" % h, align_bytes=64) for h in range(HALVES)]
-        h_woven = {}
-        hids = {}
+        hid_codes = [
+            keep.tile([P, BANK], U32, name="h_codes%d" % half, align_bytes=64) for half in range(HALVES)
+        ]
+        hid_scales = [
+            keep.tile([P, BANK], U8, name="h_scales%d" % half, align_bytes=64) for half in range(HALVES)
+        ]
+        hid_plain = {}
+        hid_woven = {}
 
-        def gate(h, lo, hi):
-            hid = keep.tile([P, PACK, hi - lo], BF16, name="hid%d_%d" % (h, lo), align_bytes=64)
+        def apply_gate(half, lo, hi):
+            hid = keep.tile([P, PACK, hi - lo], BF16, name="hid%d_%d" % (half, lo), align_bytes=64)
             for t in range(PACK):
                 nc.vector.tensor_tensor(
-                    hid[:, t, :], a_acc[h, t][:, lo:hi], gates[h, t][:, lo:hi], MULT
+                    hid[:, t, :], a_acc[half, t][:, lo:hi], gates[half, t][:, lo:hi], MULT
                 )
-            hids[h, lo] = hid
+            hid_plain[half, lo] = hid
 
-        def weave_h(h, lo, hi):
-            hid = hids[h, lo]
-            woven = keep.tile([P, PACK * (hi - lo)], BF16, name="h_woven%d_%d" % (h, lo), align_bytes=64)
-            dst = woven[:].rearrange("p (c i t) -> p c t i", i=4, t=PACK)
-            src = hid[:].rearrange("p t (c i) -> p c t i", i=4)
-            nc.scalar.copy(dst, src)
-            h_woven[h, lo] = woven
+        def weave_hid(half, lo, hi):
+            woven = keep.tile(
+                [P, PACK * (hi - lo)], BF16, name="h_woven%d_%d" % (half, lo), align_bytes=64
+            )
+            nc.scalar.copy(
+                woven[:].rearrange("part (c i t) -> part c t i", i=LINE, t=PACK),
+                hid_plain[half, lo][:].rearrange("part t (c i) -> part c t i", i=LINE),
+            )
+            hid_woven[half, lo] = woven
 
-        def quantize_h(h, lo, hi):
+        def quantize_hid(half, lo, hi):
             nc.vector.quantize_mx(
-                out=h_codes[h][:, lo:hi].bitcast(E4M3),
-                scales=h_scales[h][:, lo:hi],
-                in_=h_woven[h, lo][:],
+                out=hid_codes[half][:, lo:hi].bitcast(E4M3),
+                scales=hid_scales[half][:, lo:hi],
+                in_=hid_woven[half, lo][:],
             )
 
-        def second(nt, h, dst):
+        def output_tile(nt, half, dst):
             acc = bank()
             nc.tensor.matmul_mx(
                 out=acc[:],
                 lhsT=w3_q[nt][0].bitcast(E4M3),
                 lhsT_scale=w3_q[nt][1],
-                rhs=h_codes[h][:].bitcast(E4M3),
-                rhs_scale=h_scales[h][:],
+                rhs=hid_codes[half][:].bitcast(E4M3),
+                rhs_scale=hid_scales[half][:],
                 start=True,
                 stop=True,
             )
-            nc.vector.tensor_tensor(dst, acc[:], p_all[h][:], MULT)
+            nc.vector.tensor_tensor(dst, acc[:], p_all[half][:], MULT)
 
-        def store_half(nt, h):
+        def store_half(nt, half):
             res = stage.tile([P, BANK], F32, name="res_half", tag="res")
-            second(nt, h, res[:])
-            nc.sync.dma_start(out[nt * P : (nt + 1) * P, h * BANK : (h + 1) * BANK], res[:])
+            output_tile(nt, half, res[:])
+            nc.sync.dma_start(out[nt * P : (nt + 1) * P, half * BANK : (half + 1) * BANK], res[:])
 
         def store_both(nt):
             res = stage.tile([P, S], F32, name="res_both", tag="res")
-            for h in range(HALVES):
-                second(nt, h, res[:, h * BANK : (h + 1) * BANK])
+            for half in range(HALVES):
+                output_tile(nt, half, res[:, half * BANK : (half + 1) * BANK])
             nc.sync.dma_start(out[nt * P : (nt + 1) * P, :], res[:])
 
-        weave_w3(0, 2)
-        for lo in (0, 256):
-            gate(0, lo, lo + 256)
-            weave_h(0, lo, lo + 256)
-        quantize_w3(0, 2)
-        quantize_h(0, 0, 256)
-        quantize_h(0, 256, 512)
-        weave_w3(2, 4)
-        gate(1, 0, 512)
-        weave_h(1, 0, 512)
-        weave_w3(4, 8)
-        weave_w3(8, 12)
+        first_a = (0, TILES_PER_LOAD // 2)
+        first_b = (TILES_PER_LOAD // 2, TILES_PER_LOAD)
+        second = (TILES_PER_LOAD, 2 * TILES_PER_LOAD)
+        third = (2 * TILES_PER_LOAD, ROW_TILES)
+
+        weave_w3(*first_a)
+        for lo in range(0, BANK, PIECE):
+            apply_gate(0, lo, lo + PIECE)
+            weave_hid(0, lo, lo + PIECE)
+        quantize_w3(*first_a)
+        for lo in range(0, BANK, PIECE):
+            quantize_hid(0, lo, lo + PIECE)
+        weave_w3(*first_b)
+        apply_gate(1, 0, BANK)
+        weave_hid(1, 0, BANK)
+        weave_w3(*second)
+        weave_w3(*third)
+
         store_half(0, 0)
-        quantize_w3(2, 4)
-        for nt in range(1, 4):
+        quantize_w3(*first_b)
+        for nt in range(1, TILES_PER_LOAD):
             store_half(nt, 0)
-        quantize_h(1, 0, 512)
-        for nt in range(4):
+        quantize_hid(1, 0, BANK)
+        for nt in range(TILES_PER_LOAD):
             store_half(nt, 1)
-        quantize_w3(4, 8)
-        store_both(4)
-        store_both(5)
-        quantize_w3(8, 12)
-        for nt in range(6, 11):
+
+        quantize_w3(*second)
+        halfway = (second[0] + second[1]) // 2
+        for nt in range(second[0], halfway):
             store_both(nt)
-        for h in range(HALVES):
-            store_half(11, h)
+        quantize_w3(*third)
+        for nt in range(halfway, ROW_TILES - 1):
+            store_both(nt)
+        for half in range(HALVES):
+            store_half(ROW_TILES - 1, half)

from contextlib import ExitStack

import concourse.mybir as mybir
from concourse.masks import make_identity

K, H, N, T, S = 1536, 512, 1536, 4096, 1024
FLOPS = 2 * S * (2 * K * H + H * N)

F32 = mybir.dt.float32
BF16 = mybir.dt.bfloat16
I32 = mybir.dt.int32
U32 = mybir.dt.uint32
U16 = mybir.dt.uint16
U8 = mybir.dt.uint8
E4M3 = mybir.dt.float8_e4m3fn_x4
E5M2 = mybir.dt.float8_e5m2_x4
MULT = mybir.AluOpType.mult
SIGMOID = mybir.ActivationFunctionType.Sigmoid

P = 128
PACK = 4
K_PASS = P * PACK
PASSES = K // K_PASS
BANK = 512
HALVES = S // BANK
QUADRANTS = 4
SCALE_ROWS = 4
LINE = 4
LIST_COLS = BANK // 16
ROW_TILES = N // P
TILES_PER_LOAD = BANK // P
W3_LOADS = N // BANK

SCALE_ROW0 = [32, 48, 80]

UNIT = 8192
WIN_AT = 2 * UNIT - T // 2
TAB_AT = [4 * UNIT, 0, 2 * UNIT]
W1_AT = [4 * UNIT, 0, UNIT]
W3_AT = [2 * UNIT, 3 * UNIT, 4 * UNIT]

W1_VECTOR_SHARE = 88
PIECE = BANK // 2
LATE_GATES = 2


def tile_list_gated_expert_backward_kernel(
    tc, tab_words, tab_scales, offs, w1, w2_words, w2_scales, bg, w3, p, out
):
    nc = tc.nc
    with ExitStack() as ctx:
        keep = ctx.enter_context(tc.tile_pool(name="keep", bufs=1))
        stream = ctx.enter_context(tc.tile_pool(name="stream", bufs=1))
        work = ctx.enter_context(tc.tile_pool(name="work", bufs=2))
        stage = ctx.enter_context(tc.tile_pool(name="stage", bufs=8))
        psum = ctx.enter_context(tc.psum_pool(name="psum", bufs=8))

        def bank():
            return psum.tile([P, BANK], F32, name="bank")

        offsets = keep.tile([P, S // 16], U16, name="offsets")
        nc.sync.dma_start(offsets[:], offs)

        scale_rows = tab_scales.rearrange("a q tok -> (a q) tok").bitcast(I32)
        scale_win = stream.tile([P, T], U8, name="scale_win", align_bytes=64, offset=WIN_AT)
        scale_win_i = scale_win[:].bitcast(I32)
        nc.sync.dma_start(scale_win_i[32:64, :], scale_rows[0:32, :])
        nc.sync.dma_start(scale_win_i[80:96, :], scale_rows[32:48, :])

        w2_sraw = keep.tile([P, PASSES * H], U8, name="w2_sraw", align_bytes=64)
        nc.gpsimd.memset(w2_sraw[:].bitcast(I32), 0)
        for quad in range(QUADRANTS):
            nc.sync.dma_start(
                w2_sraw[:].bitcast(I32).rearrange("part (a c) -> part a c", a=PASSES)[
                    32 * quad : 32 * quad + SCALE_ROWS
                ],
                w2_scales.bitcast(I32)[:, SCALE_ROWS * quad : SCALE_ROWS * (quad + 1), :].rearrange(
                    "a row c -> row a c"
                ),
            )
        nc.vector.memset(scale_win_i[0:32, :], 0)
        nc.vector.memset(scale_win_i[64:80, :], 0)
        nc.gpsimd.memset(scale_win_i[96:128, :], 0)
        v_scales = keep.tile([P, PASSES * S], U8, name="v_scales", align_bytes=64)
        nc.gpsimd.memset(v_scales[:].bitcast(I32), 0)

        ident = keep.tile([P, P], F32, name="ident")
        make_identity(nc, ident[:])
        p_cols = keep.tile([P, HALVES, PACK], F32, name="p_cols")
        nc.gpsimd.dma_start(p_cols[:], p.rearrange("(half part c) -> part half c", half=HALVES, c=PACK))
        bias = keep.tile([P, PACK], F32, name="bias")
        nc.gpsimd.dma_start(bias[:], bg.rearrange("(m t) -> m t", t=PACK))

        tabs = []

        def load_table(a):
            tab = stream.tile([P, T], U32, name="tab%d" % a, align_bytes=64, offset=TAB_AT[a])
            nc.sync.dma_start(
                tab[:].bitcast(I32), tab_words[a].rearrange("part tok i -> part (tok i)").bitcast(I32)
            )
            tabs.append(tab)

        load_table(0)
        w2_raw = keep.tile([P, PASSES, H], I32, name="w2_raw", align_bytes=64)
        nc.sync.dma_start(w2_raw[:], w2_words.rearrange("a part c i -> part a (c i)").bitcast(I32))

        picked = keep.tile([P, S], U8, name="picked", align_bytes=64)
        nc.vector.tensor_copy(picked[:], scale_win[:].indirect(offsets[:]))
        for a in range(PASSES):
            for quad in range(QUADRANTS):
                row = SCALE_ROW0[a] + SCALE_ROWS * quad
                nc.sync.dma_start(
                    v_scales[:].bitcast(I32)[
                        32 * quad : 32 * quad + SCALE_ROWS, a * S // 4 : (a + 1) * S // 4
                    ],
                    picked[:].bitcast(I32)[row : row + SCALE_ROWS, :],
                )
            if a + 1 < PASSES:
                load_table(a + 1)

        p_all = []
        for half in range(HALVES):
            spread = bank()
            for c in range(PACK):
                nc.tensor.transpose(
                    spread[:, c * P : (c + 1) * P],
                    p_cols[:, half, c : c + 1].to_broadcast([P, P]),
                    ident[:],
                )
            p_half = keep.tile([P, BANK], F32, name="p_all%d" % half)
            nc.scalar.copy(
                p_half[:].rearrange("part (n c) -> part n c", c=PACK),
                spread[:].rearrange("part (c n) -> part n c", c=PACK),
            )
            p_all.append(p_half)

        w2_codes = keep.tile([P, PASSES * H], I32, name="w2_codes", align_bytes=64)
        nc.vector.tensor_copy(
            w2_codes[:].rearrange("part (a t m) -> part a m t", a=PASSES, t=PACK),
            w2_raw[:].rearrange("part a (m t) -> part a m t", t=PACK),
        )
        w2_sc = keep.tile([P, PASSES * H], U8, name="w2_sc", align_bytes=64)
        nc.vector.tensor_copy(
            w2_sc[:].rearrange("part (a t m) -> part a m t", a=PASSES, t=PACK),
            w2_sraw[:].rearrange("part (a m t) -> part a m t", a=PASSES, t=PACK),
        )

        v_codes = {}

        def gather(a, halves):
            words = keep.tile(
                [P, BANK * len(halves)], U32, name="v%d_%d" % (a, halves[0]), align_bytes=64
            )
            entries = slice(halves[0] * LIST_COLS, (halves[-1] + 1) * LIST_COLS)
            nc.vector.tensor_copy(words[:], tabs[a][:].indirect(offsets[:, entries]))
            for place, half in enumerate(halves):
                v_codes[a, half] = words[:, place * BANK : (place + 1) * BANK]

        def table_pass(acc, codes, scales, a, half):
            nc.tensor.matmul_mx(
                out=acc[:],
                lhsT=codes.bitcast(E4M3),
                lhsT_scale=scales,
                rhs=v_codes[a, half].bitcast(E5M2),
                rhs_scale=v_scales[:, a * S + half * BANK : a * S + (half + 1) * BANK],
                start=(a == 0),
                stop=(a == PASSES - 1),
            )

        b_acc = {}
        gates = {}

        def sigmoid(half, t):
            name = "gate%d_%d" % (half, t)
            if half == HALVES - 1 and t >= LATE_GATES:
                at = W1_AT[PASSES - 1] + (t - LATE_GATES) * BANK * 4
                gate = stream.tile([P, BANK], F32, name=name, align_bytes=64, offset=at)
            else:
                gate = keep.tile([P, BANK], F32, name=name)
            nc.scalar.activation(gate[:], b_acc[half, t][:], SIGMOID, bias=bias[:, t : t + 1])
            gates[half, t] = gate

        for a in range(PASSES):
            if a < PASSES - 1:
                gather(a, list(range(HALVES)))
            else:
                for half in range(HALVES):
                    gather(a, [half])
            for half in range(HALVES):
                for t in range(PACK):
                    if a == 0:
                        b_acc[half, t] = bank()
                    cols = slice(a * H + t * P, a * H + (t + 1) * P)
                    table_pass(b_acc[half, t], w2_codes[:, cols], w2_sc[:, cols], a, half)
        for t in range(PACK):
            sigmoid(0, t)

        a_acc = {}
        w1_q = []

        def hidden_pass(a, half):
            codes, scales = w1_q[a]
            for t in range(PACK):
                if a == 0:
                    a_acc[half, t] = bank()
                cols = slice(t * P, (t + 1) * P)
                table_pass(a_acc[half, t], codes[:, cols], scales[:, cols], a, half)

        for a in range(PASSES):
            last = a == PASSES - 1
            woven = work.tile([P, PACK * H], BF16, name="w1_woven", align_bytes=64)
            dst = woven[:].rearrange("part (t m j) -> part m j t", t=PACK, j=PACK)
            raw = stream.tile([P, PACK, H], F32, name="w1_raw%d" % a, align_bytes=64, offset=W1_AT[a])
            nc.sync.dma_start(
                raw[:], w1[a * K_PASS : (a + 1) * K_PASS, :].rearrange("(part j) c -> part j c", j=PACK)
            )
            src = raw[:].rearrange("part j (m t) -> part m j t", t=PACK)
            if last:
                for t in range(LATE_GATES):
                    sigmoid(1, t)
                nc.vector.tensor_copy(dst[:, :W1_VECTOR_SHARE], src[:, :W1_VECTOR_SHARE])
                nc.scalar.copy(dst[:, W1_VECTOR_SHARE:], src[:, W1_VECTOR_SHARE:])
                for t in range(LATE_GATES, PACK):
                    sigmoid(1, t)
            else:
                nc.vector.tensor_copy(dst, src)
            codes = keep.tile([P, H], U32, name="w1_codes%d" % a, align_bytes=64)
            scales = keep.tile([P, H], U8, name="w1_scales%d" % a, align_bytes=64)
            width = H // 2 if last else H
            for c0 in range(0, H, width):
                nc.vector.quantize_mx(
                    out=codes[:, c0 : c0 + width].bitcast(E4M3),
                    scales=scales[:, c0 : c0 + width],
                    in_=woven[:, c0 * PACK : (c0 + width) * PACK],
                )
            w1_q.append((codes, scales))
            hidden_pass(a, 0)
        for a in range(PASSES):
            hidden_pass(a, 1)

        w3_raw = []
        for g in range(W3_LOADS):
            raw = stream.tile([P, PACK, BANK], F32, name="w3_raw%d" % g, align_bytes=64, offset=W3_AT[g])
            nc.sync.dma_start(
                raw[:], w3.rearrange("(part j) n -> part j n", j=PACK)[:, :, g * BANK : (g + 1) * BANK]
            )
            w3_raw.append(raw)

        w3_woven = {}
        w3_q = {}

        def weave_w3(lo, hi):
            woven = keep.tile([P, PACK * (hi - lo) * P], BF16, name="w3_woven%d" % lo, align_bytes=64)
            first = (lo % TILES_PER_LOAD) * P
            src = w3_raw[lo // TILES_PER_LOAD][:, :, first : first + (hi - lo) * P]
            nc.scalar.copy(
                woven[:].rearrange("part (c i j) -> part c j i", i=LINE, j=PACK),
                src.rearrange("part j (c i) -> part c j i", i=LINE),
            )
            w3_woven[lo] = woven

        def quantize_w3(lo, hi):
            codes = keep.tile([P, (hi - lo) * P], U32, name="w3_codes%d" % lo, align_bytes=64)
            scales = keep.tile([P, (hi - lo) * P], U8, name="w3_scales%d" % lo, align_bytes=64)
            nc.vector.quantize_mx(out=codes[:].bitcast(E4M3), scales=scales[:], in_=w3_woven[lo][:])
            for nt in range(lo, hi):
                cols = slice((nt - lo) * P, (nt - lo + 1) * P)
                w3_q[nt] = (codes[:, cols], scales[:, cols])

        hid_codes = [
            keep.tile([P, BANK], U32, name="h_codes%d" % half, align_bytes=64) for half in range(HALVES)
        ]
        hid_scales = [
            keep.tile([P, BANK], U8, name="h_scales%d" % half, align_bytes=64) for half in range(HALVES)
        ]
        hid_plain = {}
        hid_woven = {}

        def apply_gate(half, lo, hi):
            hid = keep.tile([P, PACK, hi - lo], BF16, name="hid%d_%d" % (half, lo), align_bytes=64)
            for t in range(PACK):
                nc.vector.tensor_tensor(
                    hid[:, t, :], a_acc[half, t][:, lo:hi], gates[half, t][:, lo:hi], MULT
                )
            hid_plain[half, lo] = hid

        def weave_hid(half, lo, hi):
            woven = keep.tile(
                [P, PACK * (hi - lo)], BF16, name="h_woven%d_%d" % (half, lo), align_bytes=64
            )
            nc.scalar.copy(
                woven[:].rearrange("part (c i t) -> part c t i", i=LINE, t=PACK),
                hid_plain[half, lo][:].rearrange("part t (c i) -> part c t i", i=LINE),
            )
            hid_woven[half, lo] = woven

        def quantize_hid(half, lo, hi):
            nc.vector.quantize_mx(
                out=hid_codes[half][:, lo:hi].bitcast(E4M3),
                scales=hid_scales[half][:, lo:hi],
                in_=hid_woven[half, lo][:],
            )

        def output_tile(nt, half, dst):
            acc = bank()
            nc.tensor.matmul_mx(
                out=acc[:],
                lhsT=w3_q[nt][0].bitcast(E4M3),
                lhsT_scale=w3_q[nt][1],
                rhs=hid_codes[half][:].bitcast(E4M3),
                rhs_scale=hid_scales[half][:],
                start=True,
                stop=True,
            )
            nc.vector.tensor_tensor(dst, acc[:], p_all[half][:], MULT)

        def store_half(nt, half):
            res = stage.tile([P, BANK], F32, name="res_half", tag="res")
            output_tile(nt, half, res[:])
            nc.sync.dma_start(out[nt * P : (nt + 1) * P, half * BANK : (half + 1) * BANK], res[:])

        def store_both(nt):
            res = stage.tile([P, S], F32, name="res_both", tag="res")
            for half in range(HALVES):
                output_tile(nt, half, res[:, half * BANK : (half + 1) * BANK])
            nc.sync.dma_start(out[nt * P : (nt + 1) * P, :], res[:])

        first_a = (0, TILES_PER_LOAD // 2)
        first_b = (TILES_PER_LOAD // 2, TILES_PER_LOAD)
        second = (TILES_PER_LOAD, 2 * TILES_PER_LOAD)
        third = (2 * TILES_PER_LOAD, ROW_TILES)

        weave_w3(*first_a)
        for lo in range(0, BANK, PIECE):
            apply_gate(0, lo, lo + PIECE)
            weave_hid(0, lo, lo + PIECE)
        quantize_w3(*first_a)
        for lo in range(0, BANK, PIECE):
            quantize_hid(0, lo, lo + PIECE)
        weave_w3(*first_b)
        apply_gate(1, 0, BANK)
        weave_hid(1, 0, BANK)
        weave_w3(*second)
        weave_w3(*third)

        store_half(0, 0)
        quantize_w3(*first_b)
        for nt in range(1, TILES_PER_LOAD):
            store_half(nt, 0)
        quantize_hid(1, 0, BANK)
        for nt in range(TILES_PER_LOAD):
            store_half(nt, 1)

        quantize_w3(*second)
        halfway = (second[0] + second[1]) // 2
        for nt in range(second[0], halfway):
            store_both(nt)
        quantize_w3(*third)
        for nt in range(halfway, ROW_TILES - 1):
            store_both(nt)
        for half in range(HALVES):
            store_half(ROW_TILES - 1, half)
